import numpy as np, ml_dtypes
CORES = [5,29,101,125,133,157,229,253]
N = 8
import mx_ref
BF = ml_dtypes.bfloat16
def entries(a):
    return np.ascontiguousarray(a.T).reshape(-1)
def table(e):
    return np.ascontiguousarray(np.reshape(e, (-1, 16)).T).astype(np.int32)
def cols(t, e):
    v = np.concatenate([t.reshape(128, -1, 4), np.zeros((128, 1, 4), BF)], axis=1)
    return np.ascontiguousarray(v[:, e]).reshape(128, -1)
def f(rng, *shape):
    return mx_ref.flush((rng.standard_normal(shape, dtype=np.float32) * np.exp2(rng.integers(-2, 3, shape[:-1] + (1,)))).astype(BF))
def wide(rng, *shape, cols=0):
    v = rng.standard_normal(shape, dtype=np.float32) * np.exp2(rng.integers(-12, 13, shape)).astype(np.float32)
    if cols: v *= np.repeat(np.exp2(rng.integers(-cols, cols + 1, shape[:-2] + (1, shape[-1] // 4))) * (rng.random(shape[:-2] + (1, shape[-1] // 4)) > 0.0625), 4, axis=-1).astype(np.float32)
    return mx_ref.flush(v.astype(BF))
T, W, UN, CR = 512, 512, 160, 80
HOST = [0 if k < 128 else 1 for k in CORES]
def lists(rng, full=False, alike=False):
    uni, need, pos = np.full((N, 2, UN), -1), np.full((N, N, CR), -1), []
    for q in range(N):
        for g in range(2):
            mates = [r for r in range(N) if HOST[r] == g]
            n = UN if full else int(rng.integers(CR >> 1, CR + 1)) if alike else int(rng.integers(UN >> 2, UN + 1))
            at = rng.permutation(UN)[:n]
            uni[q, g, at] = rng.permutation(T)[:n]
            who = rng.permutation(np.repeat(np.arange(len(mates)), CR))[:n]
            for i, r in enumerate(mates):
                e, others = at[who == i], at[who != i]
                if alike: e = at
                else:
                    k = CR if full else int(rng.integers(max(len(e), CR >> 2), min(CR, n) + 1))
                    e = np.concatenate([e, rng.permutation(others)[:k - len(e)]])
                need[r, q, rng.permutation(CR)[:len(e)]] = e
    for r in range(N):
        ok = np.flatnonzero(need[r].reshape(-1) >= 0)
        pos.append(table(rng.permutation(ok)[:W] if full else rng.choice(ok, W)))
    return {"uni": np.stack([table(e.reshape(-1)) for e in uni]), "need": np.stack([table(e.reshape(-1)) for e in need]), "pos": np.stack(pos)}
def setup_inputs(rng):
    return {"c": f(rng, N, 128, 4 * T), "w": f(rng, N, 128, 512), **lists(rng)}
def setup_inputs_alike(rng):
    return {**setup_inputs(rng), **lists(rng, alike=True)}
def setup_inputs_pairs(rng):
    d = setup_inputs(rng)
    uni, need = np.full((N, 2, UN), -1), np.full((N, N, CR), -1)
    for g in range(2):
        mates = rng.permutation([r for r in range(N) if HOST[r] == g])
        for q in range(N):
            at = rng.permutation(UN)[:2 * CR]
            uni[q, g, at] = rng.permutation(T)[:2 * CR]
            for i, r in enumerate(mates):
                need[r, q] = rng.permutation(at[:CR] if i < len(mates) // 2 else at[CR:])
    pos = [table(rng.choice(N * CR, W)) for r in range(N)]
    return {**d, "uni": np.stack([table(e.reshape(-1)) for e in uni]), "need": np.stack([table(e.reshape(-1)) for e in need]), "pos": np.stack(pos)}
def setup_inputs_full(rng):
    return {**setup_inputs(rng), **lists(rng, full=True)}
def setup_inputs_few(rng):
    d = {**setup_inputs(rng), **lists(rng, full=True)}
    uni = np.stack([entries(e) for e in d["uni"]]).reshape(N, 2, UN)
    need = np.stack([entries(e) for e in d["need"]]).reshape(N, N, CR)
    pos = [None] * N
    for g in range(2):
        p = rng.permutation(N)
        h = [HOST[q] for q in p]
        lead = [h.index(0), h.index(1)]
        own = np.concatenate([p[lead], np.delete(p, lead)])[:-(-W // CR)]
        rest = np.setdiff1d(np.arange(N), own)
        uni[rest, g] = -1
        for r in range(N):
            if HOST[r] != g: continue
            need[r, rest] = -1
            s = rng.permutation(own)[:, None] * CR + np.arange(CR)
            s[-1] = rng.permutation(s[-1])
            pos[r] = table(rng.permutation(s.reshape(-1)[:W]))
    return {**d, "uni": np.stack([table(e.reshape(-1)) for e in uni]), "need": np.stack([table(e.reshape(-1)) for e in need]), "pos": np.stack(pos)}
def setup_inputs_spread(rng):
    d = setup_inputs(rng); d["c"] = wide(rng, N, 128, 4 * T, cols=6); return d
def check_inputs(d):
    b = []
    uni = np.stack([entries(e) for e in d["uni"]]).reshape(N, 2, UN)
    need = np.stack([entries(e) for e in d["need"]]).reshape(N, N, CR)
    if uni.min() < -1 or uni.max() >= T: b.append("uni")
    if need.min() < -1 or need.max() >= UN: return b + ["need"]
    for q in range(N):
        for g in range(2):
            e = uni[q, g][uni[q, g] >= 0]
            if len(set(e.tolist())) != len(e): b.append("a column of one owner twice for one host")
            named = set()
            for r in range(N):
                if HOST[r] != g: continue
                k = need[r, q][need[r, q] >= 0]
                if len(set(k.tolist())) != len(k): b.append("need names an entry of one union twice")
                if (uni[q, g][k] < 0).any(): b.append("need names an empty entry of uni")
                named |= set(k.tolist())
            if set(np.flatnonzero(uni[q, g] >= 0).tolist()) - named: b.append("an entry of uni that no rank of the host needs")
    for r in range(N):
        p = entries(d["pos"][r])
        if p.min() < 0 or p.max() >= N * CR or (need[r].reshape(-1)[p] < 0).any(): b.append("pos")
    return b
def reference(c, w, uni, need, pos):
    uni = np.stack([entries(e) for e in uni]).reshape(N, 2, UN)
    need = np.stack([entries(e) for e in need]).reshape(N, N, CR)
    y = np.zeros((N, 128, W), np.float32)
    for r in range(N):
        g = HOST[r]
        t = np.concatenate([cols(c[q], np.where(need[r, q] >= 0, uni[q, g][need[r, q]], -1)) for q in range(N)], axis=1)
        y[r] = mx_ref.matmul(mx_ref.quantize(w[r]), mx_ref.quantize(cols(t, entries(pos[r]))))
    return {"y": y}

@@ -1,0 +1,279 @@
+from concourse.bass import DstId, RemoteDMATransfer
+from concourse.mybir import dt, AluOpType, ActivationFunctionType
+
+N, UN, CR, T_COLS, W = 8, 160, 80, 512, 512
+PER = 4
+BLK = 2 * CR
+LU, LN = UN // 16, CR // 16
+K = 2 * LN
+CODES, I32, U16, F32 = "float8_e4m3fn_x4", "int32", "uint16", "float32"
+
+SCRATCH = {
+    "needs": ("sbuf", [128, N, LN], I32),
+    "nlist": ("sbuf", [128, PER, K], U16),
+    "nown": ("sbuf", [128, K], U16),
+    "nland": ("sbuf", [128, 3 * K], U16),
+    "unis": ("sbuf", [128, 2 * LU], I32),
+    "uoff": ("sbuf", [128, 2 * LU], U16),
+    "poff": ("sbuf", [128, W // 16], U16),
+    "ct": ("sbuf", [128, 4 * T_COLS], "bfloat16"),
+    "wt": ("sbuf", [128, 512], "bfloat16"),
+    "cq": ("sbuf", [128, T_COLS], CODES),
+    "cs": ("sbuf", [128, T_COLS], "uint8"),
+    "wq": ("sbuf", [128, 128], CODES),
+    "ws": ("sbuf", [128, 128], "uint8"),
+    "xq": ("sbuf", [128, UN], CODES),
+    "xs": ("sbuf", [128, UN], "uint8"),
+    "winq": ("sbuf", [128, 2 * UN], CODES),
+    "wins": ("sbuf", [128, 2 * UN], "uint8"),
+    "vq": ("sbuf", [128, 3 * BLK], CODES),
+    "vs": ("sbuf", [128, 3 * BLK], "uint8"),
+    "landq": ("sbuf", [128, PER * BLK], CODES),
+    "lands": ("sbuf", [128, PER * BLK], "uint8"),
+    "hn": ("sbuf", [128, K], U16),
+    "hp": ("sbuf", [128, LN], U16),
+    "hq": ("sbuf", [128, BLK], CODES),
+    "hs": ("sbuf", [128, BLK], "uint8"),
+    "ps": ("psum", [128, 512 * PER], F32),
+    "res": ("sbuf", [128, PER * BLK], F32),
+    "yt": ("sbuf", [128, W], F32),
+}
+for n_ in ("poss", "pa", "pb", "b1", "b2", "b3", "b4", "s1", "s2", "s3"):
+    SCRATCH[n_] = ("sbuf", [128, W // 16], I32)
+PEERS = ["near", "far", "par"]
+SEMAPHORES = (["ld_need", "ld_uni", "ld_c0", "ld_c1", "ld_w", "ld_pos", "sent",
+               "v_n0", "v_n1", "v_o0", "v_o1", "v_u", "v_qc", "v_qw", "v_xq", "a_xs", "v_wq", "a_ws",
+               "x_q", "x_s", "h_n", "h_d",
+               "v_p0", "v_p1", "v_p2", "v_p3", "v_p4", "v_p5", "v_p6", "v_p7", "v_p8", "v_p9", "v_po",
+               "v_me", "a_me", "v_y0", "a_y0", "v_y1", "a_y1", "st0", "st1"]
+              + [x + p for x in ("n_", "q_", "s_", "v_", "a_") for p in PEERS]
+              + ["mm%d" % b for b in range(4)] + ["cp%d" % b for b in range(4)])
+
+
+def mask_of(engines):
+    return sum(1 << e for e in engines)
+
+
+def plan(T, topo, r):
+    me = T.cores[r]
+    mates = [q for q in range(N) if topo.host(T.cores[q]) == topo.host(me) and q != r]
+    par = [q for q in mates if topo.may_write(me, T.cores[q])][0]
+    near = r ^ 1
+    far = [q for q in mates if q not in (par, near)][0]
+    own = [c for c in topo.cores_of(me) if c != me]
+    hnear = [c for c in own if topo.may_write(c, T.cores[near]) and topo.die(c) == topo.die(me)][:2]
+    hfar = [c for c in own if topo.may_write(c, T.cores[far]) and topo.die(c) != topo.die(me)][:2]
+    return {"near": near, "far": far, "par": par, "hnear": hnear, "hfar": hfar}
+
+
+def helper_program(g, core, T, topo, r, role, pl):
+    S = T.sem
+    dst, par = T.cores[pl[role]], T.cores[pl["par"]]
+    rid, pid = topo.addr(dst, core)
+    m = mask_of(topo.engines(core, dst)[:8])
+    b = (r % PER) * BLK
+    slot = PEERS.index(role) * K
+    if core == pl["h" + role][0]:
+        g.wait_ge(S.h_n, 8)
+        g.remote_dma(T.nland[:, slot:slot + K], T.hn[:], S["n_" + role], S.sent, pid, rid, m)
+        g.wait_ge(S.h_d, 16)
+        g.remote_dma(T.landq[:, b:b + BLK].bitcast(dt.uint8), T.hq[:, 0:BLK].bitcast(dt.uint8), S["q_" + role], S.sent, pid, rid, m)
+    else:
+        prid, ppid = topo.addr(par, core)
+        e = 2 * K + (0 if role == "near" else LN)
+        g.wait_ge(S.h_n, 4)
+        g.remote_dma(T.nland[:, e:e + LN], T.hp[:], S.n_par, S.sent, ppid, prid, mask_of(topo.engines(core, par)[:8]))
+        g.wait_ge(S.h_d, 8)
+        g.remote_dma(T.lands[:, b:b + BLK], T.hs[:, 0:BLK], S["s_" + role], S.sent, pid, rid, m)
+    g.wait_ge(S.sent, 16)
+
+
+def rank_program(g, core, T, topo):
+    r = T.rank_of(core)
+    if r is None:
+        for q in range(N):
+            if core in topo.cores_of(T.cores[q]):
+                pl = plan(T, topo, q)
+                for role in ("near", "far"):
+                    if core in pl["h" + role]:
+                        helper_program(g, core, T, topo, q, role, pl)
+        return
+    S = T.sem
+    v, a, te, sy = g.vector, g.scalar, g.tensor, g.sync
+    COPY = ActivationFunctionType.Copy
+    pl = plan(T, topo, r)
+    h, b = r // PER, r % PER
+    own0 = h * UN
+    xh = T.cores[(r + PER) % N]
+
+    for i in range(8):
+        (sy if i % 2 == 0 else a).dma_start(T.needs[16 * i:16 * i + 16, :, :], T.need[:]).then_inc(S.ld_need, 16)
+    for i in range(2):
+        a.dma_start(T.ct[:, 2 * T_COLS * i:2 * T_COLS * (i + 1)], T.c[:, 2 * T_COLS * i:2 * T_COLS * (i + 1)]).then_inc(S["ld_c%d" % i], 16)
+    for i in range(8):
+        (sy if i % 2 == 0 else a).dma_start(T.unis[16 * i:16 * i + 16, :], T.uni[:]).then_inc(S.ld_uni, 16)
+    sy.wait_ge(S.ld_need, 128)
+    sy.dma_start(T.wt[:], T.w[:]).then_inc(S.ld_w, 16)
+    for i in range(8):
+        sy.dma_start(T.poss[16 * i:16 * i + 16, :], T.pos[:]).then_inc(S.ld_pos, 16)
+
+    def offs(who):
+        if who == "me":
+            return T.nown[:, 0:K]
+        e = PEERS.index(who) * K
+        return T.nland[:, e:e + K]
+
+    def place(who):
+        return (b if who == "me" else PEERS.index(who)) * BLK
+
+    def pick_codes(who):
+        p, out = place(who), T.landq if who == "me" else T.vq
+        v.tensor_copy(out[:, p:p + BLK].bitcast(dt.uint32), T.winq[:, 0:2 * UN].bitcast(dt.uint32).indirect(offs(who))).then_inc(S["v_" + who], 1)
+
+    def pick_scales(who):
+        p, out = place(who), T.lands if who == "me" else T.vs
+        a.activation(out[:, p:p + BLK], T.wins[:, 0:2 * UN].indirect(offs(who)), COPY).then_inc(S["a_" + who], 1)
+
+    v.wait_ge(S.ld_need, 128)
+    v.tensor_copy(T.nlist[:, :, 0:LN], T.needs[:, 0:PER, :]).then_inc(S.v_n0, 1)
+    v.tensor_scalar(T.nlist[:, :, LN:K], T.needs[:, PER:N, :], float(UN), None, AluOpType.add).then_inc(S.v_n1, 1)
+    hc = T_COLS // 2
+    v.wait_ge(S.ld_c0, 16)
+    v.quantize_mx(T.cq[:, 0:hc], T.cs[:, 0:hc], T.ct[:, 0:4 * hc]).then_inc(S.v_qc, 1)
+    v.wait_ge(S.ld_uni, 128)
+    v.tensor_copy(T.uoff[:], T.unis[:]).then_inc(S.v_u, 1)
+    v.wait_ge(S.ld_c1, 16)
+    v.quantize_mx(T.cq[:, hc:T_COLS], T.cs[:, hc:T_COLS], T.ct[:, 4 * hc:4 * T_COLS]).then_inc(S.v_qc, 1)
+    uoth, uown = T.uoff[:, (1 - h) * LU:(2 - h) * LU], T.uoff[:, h * LU:(h + 1) * LU]
+    v.wait_ge(S.v_u, 1)
+    v.wait_ge(S.v_qc, 2)
+    v.tensor_copy(T.xq[:, 0:UN].bitcast(dt.uint32), T.cq[:, 0:T_COLS].bitcast(dt.uint32).indirect(uoth)).then_inc(S.v_xq, 1)
+    v.tensor_copy(T.winq[:, own0:own0 + UN].bitcast(dt.uint32), T.cq[:, 0:T_COLS].bitcast(dt.uint32).indirect(uown)).then_inc(S.v_wq, 1)
+    v.tensor_copy(T.nown[:, 0:LN], T.needs[:, b, :]).then_inc(S.v_o0, 1)
+    v.tensor_scalar(T.nown[:, LN:K], T.needs[:, PER + b, :], float(UN), None, AluOpType.add).then_inc(S.v_o1, 1)
+    v.wait_ge(S.v_wq, 1)
+    v.wait_ge(S.x_q, 8)
+    v.wait_ge(S.n_near, 8)
+    pick_codes("near")
+    v.wait_ge(S.n_far, 8)
+    pick_codes("far")
+    v.wait_ge(S.n_par, 16)
+    pick_codes("par")
+    v.wait_ge(S.v_o0, 1)
+    v.wait_ge(S.v_o1, 1)
+    pick_codes("me")
+    v.wait_ge(S.ld_w, 16)
+    v.quantize_mx(T.wq[:, 0:128], T.ws[:, 0:128], T.wt[:, 0:512]).then_inc(S.v_qw, 1)
+    GE, MUL, ADD = AluOpType.is_ge, AluOpType.mult, AluOpType.add
+    v.wait_ge(S.ld_pos, 128)
+    v.tensor_scalar(T.pa[:], T.poss[:], float(PER * CR), float(PER * CR), GE, MUL).then_inc(S.v_p0, 1)
+    v.tensor_scalar(T.b4[:], T.poss[:], float(PER * CR), float(CR), GE, MUL).then_inc(S.v_p1, 1)
+    v.wait_ge(S.v_p0, 1)
+    v.tensor_tensor(T.pb[:], T.poss[:], T.pa[:], AluOpType.subtract).then_inc(S.v_p2, 1)
+    v.wait_ge(S.v_p2, 1)
+    v.tensor_scalar(T.b1[:], T.pb[:], float(CR), float(CR), GE, MUL).then_inc(S.v_p3, 1)
+    v.tensor_scalar(T.b2[:], T.pb[:], float(2 * CR), float(CR), GE, MUL).then_inc(S.v_p4, 1)
+    v.tensor_scalar(T.b3[:], T.pb[:], float(3 * CR), float(CR), GE, MUL).then_inc(S.v_p5, 1)
+    v.wait_ge(S.v_p3, 1)
+    v.wait_ge(S.v_p4, 1)
+    v.tensor_tensor(T.s1[:], T.b1[:], T.b2[:], ADD).then_inc(S.v_p6, 1)
+    v.wait_ge(S.v_p1, 1)
+    v.wait_ge(S.v_p5, 1)
+    v.tensor_tensor(T.s2[:], T.b3[:], T.b4[:], ADD).then_inc(S.v_p7, 1)
+    v.wait_ge(S.v_p6, 1)
+    v.wait_ge(S.v_p7, 1)
+    v.tensor_tensor(T.s3[:], T.s1[:], T.s2[:], ADD).then_inc(S.v_p8, 1)
+    v.wait_ge(S.v_p8, 1)
+    v.tensor_tensor(T.pa[:], T.s3[:], T.pb[:], ADD).then_inc(S.v_p9, 1)
+    v.wait_ge(S.v_p9, 1)
+    v.tensor_copy(T.poff[:], T.pa[:]).then_inc(S.v_po, 1)
+
+    a.wait_ge(S.v_u, 1)
+    a.wait_ge(S.v_qc, 2)
+    a.activation(T.xs[:, 0:UN], T.cs[:, 0:T_COLS].indirect(uoth), COPY).then_inc(S.a_xs, 1)
+    a.activation(T.wins[:, own0:own0 + UN], T.cs[:, 0:T_COLS].indirect(uown), COPY).then_inc(S.a_ws, 1)
+    a.wait_ge(S.a_ws, 1)
+    a.wait_ge(S.x_s, 8)
+    a.wait_ge(S.n_near, 8)
+    pick_scales("near")
+    a.wait_ge(S.n_far, 8)
+    pick_scales("far")
+    a.wait_ge(S.n_par, 16)
+    pick_scales("par")
+    a.wait_ge(S.v_o0, 1)
+    a.wait_ge(S.v_o1, 1)
+    pick_scales("me")
+
+    def did(dst):
+        rid, pid = topo.addr(dst, core)
+        return [DstId(rid=rid, pnc=pid)]
+
+    hn, hf, sp = pl["hnear"], pl["hfar"], T.cores[pl["par"]]
+    en, ef = topo.engines(core, hn[0]), topo.engines(core, hf[0])
+    mp, mx = mask_of(topo.engines(core, sp)[:8]), mask_of(topo.engines(core, xh)[:8])
+    half = len(en) // 2
+    nd, fd, pd = pl["near"] % PER, pl["far"] % PER, pl["par"] % PER
+    g.wait_ge(S.v_n0, 1)
+    g.wait_ge(S.v_n1, 1)
+    for d, hc_ in ((nd, hn[0]), (fd, hf[0])):
+        hrid, hpid = topo.addr(hc_, core)
+        g.remote_dma(T.hn[:], T.nlist[:, d, :], S.h_n, S.sent, hpid, hrid, mask_of(topo.engines(core, hc_)[half:]))
+    g.remote_dma_fused([
+        RemoteDMATransfer(dst_ids=did(hn[1]), dma_engine_mask=mask_of(en[0:4]), remote_sem=S.h_n, src=T.nlist[:, pd, 0:LN], dst=T.hp[:]),
+        RemoteDMATransfer(dst_ids=did(hf[1]), dma_engine_mask=mask_of(ef[4:8]), remote_sem=S.h_n, src=T.nlist[:, pd, LN:K], dst=T.hp[:]),
+    ], local_sem=S.sent)
+    xrid, xpid = topo.addr(xh, core)
+    g.wait_ge(S.v_xq, 1)
+    g.remote_dma(T.winq[:, own0:own0 + UN].bitcast(dt.uint8), T.xq[:, 0:UN].bitcast(dt.uint8), S.x_q, S.sent, xpid, xrid, mx)
+    g.wait_ge(S.a_xs, 1)
+    g.remote_dma(T.wins[:, own0:own0 + UN], T.xs[:, 0:UN], S.x_s, S.sent, xpid, xrid, mx)
+    to = {"far": (hf, ef[half:]), "near": (hn, en[:half])}
+    for who in ("near", "far"):
+        p, hc_ = place(who), to[who][0][0]
+        hrid, hpid = topo.addr(hc_, core)
+        g.wait_ge(S["v_" + who], 1)
+        g.remote_dma(T.hq[:, 0:BLK].bitcast(dt.uint8), T.vq[:, p:p + BLK].bitcast(dt.uint8), S.h_d, S.sent, hpid, hrid, mask_of(topo.engines(core, hc_)))
+    for who in ("near", "far"):
+        p, hs_ = place(who), to[who][0][1]
+        hrid, hpid = topo.addr(hs_, core)
+        g.wait_ge(S["a_" + who], 1)
+        g.remote_dma(T.hs[:, 0:BLK], T.vs[:, p:p + BLK], S.h_d, S.sent, hpid, hrid, mask_of(to[who][1]))
+    rid, pid = topo.addr(sp, core)
+    g.wait_ge(S.v_par, 1)
+    g.remote_dma(T.landq[:, b * BLK:(b + 1) * BLK].bitcast(dt.uint8), T.vq[:, 2 * BLK:3 * BLK].bitcast(dt.uint8), S.q_par, S.sent, pid, rid, mp)
+    g.wait_ge(S.a_par, 1)
+    g.remote_dma(T.lands[:, b * BLK:(b + 1) * BLK], T.vs[:, 2 * BLK:3 * BLK], S.s_par, S.sent, pid, rid, mp)
+    g.wait_ge(S.sent, 104)
+
+    te.wait_ge(S.v_qw, 1)
+    order = [(b, None), (pd, "par"), (nd, "near"), (fd, "far")]
+    for j, role in order:
+        if role is None:
+            te.wait_ge(S.v_me, 1)
+            te.wait_ge(S.a_me, 1)
+        else:
+            te.wait_ge(S["q_" + role], 8)
+            te.wait_ge(S["s_" + role], 8)
+        te.matmul_mx(T.ps[:, 512 * j:512 * j + BLK], T.wq[:, 0:128], T.ws[:, 0:128],
+                     T.landq[:, j * BLK:(j + 1) * BLK], T.lands[:, j * BLK:(j + 1) * BLK], True, True).then_inc(S["mm%d" % j], 1)
+    for j in (b, fd):
+        v.wait_ge(S["mm%d" % j], 1)
+        v.tensor_copy(T.res[:, j * BLK:(j + 1) * BLK], T.ps[:, 512 * j:512 * j + BLK]).then_inc(S["cp%d" % j], 1)
+    for j in (pd, nd):
+        a.wait_ge(S["mm%d" % j], 1)
+        a.activation(T.res[:, j * BLK:(j + 1) * BLK], T.ps[:, 512 * j:512 * j + BLK], COPY).then_inc(S["cp%d" % j], 1)
+    for e in (v, a):
+        e.wait_ge(S.v_po, 1)
+        for j in range(PER):
+            e.wait_ge(S["cp%d" % j], 1)
+    win = T.res[:, 0:PER * BLK]
+    qw, qk = W // 4, W // 64
+    for i in range(2):
+        c0, k0 = 2 * i * qw, 2 * i * qk
+        v.tensor_copy(T.yt[:, c0:c0 + qw], win.indirect(T.poff[:, k0:k0 + qk])).then_inc(S["v_y%d" % i], 1)
+        a.activation(T.yt[:, c0 + qw:c0 + 2 * qw], win.indirect(T.poff[:, k0 + qk:k0 + 2 * qk]), COPY).then_inc(S["a_y%d" % i], 1)
+        sy.wait_ge(S["v_y%d" % i], 1)
+        sy.wait_ge(S["a_y%d" % i], 1)
+        sy.dma_start(T.y[:, c0:c0 + 2 * qw], T.yt[:, c0:c0 + 2 * qw]).then_inc(S["st%d" % i], 16)
+    for i in range(2):
+        sy.wait_ge(S["st%d" % i], 16)

@@ -3,18 +3,30 @@ from concourse.mybir import dt, AluOpType, ActivationFunctionType
 
 N, UN, CR, T_COLS, W = 8, 160, 80, 512, 512
 PER = 4
-BLK = 2 * CR
 LU, LN = UN // 16, CR // 16
-K = 2 * LN
+LP = LN + 1
 CODES, I32, U16, F32 = "float8_e4m3fn_x4", "int32", "uint16", "float32"
+C_PARTS = [(0, 256), (256, 384), (384, 512)]
+Y_STEPS = [64, 64, 128]
+MM_MIN = 128
+
+SENT = {"near": "x", "far": "x", "paro": "o", "parx": "x", "relay": "r"}
+MINE = {"meo": "o", "mex": "x", "mer": "r"}
+LAND = ["near", "meo", "paro", "far", "mer", "mex", "parx", "relay"]
+PRODUCTS = [("e", ["meo", "paro"], CR, 2 * CR), ("m", ["mer", "mex"], 4 * CR, 2 * CR),
+            ("parx", ["parx"], 7 * CR - MM_MIN, MM_MIN), ("near", ["near"], 0, MM_MIN),
+            ("far", ["far"], 4 * CR - MM_MIN, MM_MIN), ("relay", ["relay"], 8 * CR - MM_MIN, MM_MIN)]
 
 SCRATCH = {
+    "raw": ("dram", [128, LN], I32),
+    "hraw": ("dram", [128, LN], I32),
+    "praw": ("dram", [2, 128, LN], I32),
     "needs": ("sbuf", [128, N, LN], I32),
-    "nlist": ("sbuf", [128, PER, K], U16),
-    "nown": ("sbuf", [128, K], U16),
-    "nland": ("sbuf", [128, 3 * K], U16),
+    "nl": ("sbuf", [128, N, LP], U16),
+    "rels": ("sbuf", [128, LN], I32),
     "unis": ("sbuf", [128, 2 * LU], I32),
     "uoff": ("sbuf", [128, 2 * LU], U16),
+    "poss": ("sbuf", [128, W // 16], I32),
     "poff": ("sbuf", [128, W // 16], U16),
     "ct": ("sbuf", [128, 4 * T_COLS], "bfloat16"),
     "wt": ("sbuf", [128, 512], "bfloat16"),
@@ -24,34 +36,40 @@ SCRATCH = {
     "ws": ("sbuf", [128, 128], "uint8"),
     "xq": ("sbuf", [128, UN], CODES),
     "xs": ("sbuf", [128, UN], "uint8"),
-    "winq": ("sbuf", [128, 2 * UN], CODES),
-    "wins": ("sbuf", [128, 2 * UN], "uint8"),
-    "vq": ("sbuf", [128, 3 * BLK], CODES),
-    "vs": ("sbuf", [128, 3 * BLK], "uint8"),
-    "landq": ("sbuf", [128, PER * BLK], CODES),
-    "lands": ("sbuf", [128, PER * BLK], "uint8"),
-    "hn": ("sbuf", [128, K], U16),
-    "hp": ("sbuf", [128, LN], U16),
-    "hq": ("sbuf", [128, BLK], CODES),
-    "hs": ("sbuf", [128, BLK], "uint8"),
-    "ps": ("psum", [128, 512 * PER], F32),
-    "res": ("sbuf", [128, PER * BLK], F32),
+    "vq": ("sbuf", [128, len(SENT) * CR], CODES),
+    "vs": ("sbuf", [128, len(SENT) * CR], "uint8"),
+    "landq": ("sbuf", [128, N * CR], CODES),
+    "lands": ("sbuf", [128, N * CR], "uint8"),
+    "hn": ("sbuf", [128, LN], U16),
+    "hoq": ("sbuf", [128, UN], CODES),
+    "hos": ("sbuf", [128, UN], "uint8"),
+    "hq": ("sbuf", [128, CR], CODES),
+    "hs": ("sbuf", [128, CR], "uint8"),
+    "ps": ("psum", [128, 512 * len(PRODUCTS)], F32),
+    "res": ("sbuf", [128, N * CR], F32),
     "yt": ("sbuf", [128, W], F32),
 }
-for n_ in ("poss", "pa", "pb", "b1", "b2", "b3", "b4", "s1", "s2", "s3"):
-    SCRATCH[n_] = ("sbuf", [128, W // 16], I32)
-PEERS = ["near", "far", "par"]
-SEMAPHORES = (["ld_need", "ld_uni", "ld_c0", "ld_c1", "ld_w", "ld_pos", "sent",
-               "v_n0", "v_n1", "v_o0", "v_o1", "v_u", "v_qc", "v_qw", "v_xq", "a_xs", "v_wq", "a_ws",
-               "x_q", "x_s", "h_n", "h_d",
-               "v_p0", "v_p1", "v_p2", "v_p3", "v_p4", "v_p5", "v_p6", "v_p7", "v_p8", "v_p9", "v_po",
-               "v_me", "a_me", "v_y0", "a_y0", "v_y1", "a_y1", "st0", "st1"]
-              + [x + p for x in ("n_", "q_", "s_", "v_", "a_") for p in PEERS]
-              + ["mm%d" % b for b in range(4)] + ["cp%d" % b for b in range(4)])
+for n_ in "oxr":
+    SCRATCH["w%sq" % n_] = ("sbuf", [128, UN], CODES)
+    SCRATCH["w%ss" % n_] = ("sbuf", [128, UN], "uint8")
+for n_ in SENT:
+    SCRATCH["n" + n_] = ("sbuf", [128, LP], U16)
+SEMAPHORES = (["ld_raw", "ld_need", "ld_uni", "ld_w", "ld_pos", "ld_rel", "sent", "l_sent", "raw_in",
+               "v_n", "v_u", "v_rel", "v_qc", "v_qw", "v_po", "v_xq", "a_xs", "v_oq", "a_os",
+               "x_q", "x_s", "r_q", "r_s", "h_raw", "h_n", "h_o", "h_q", "h_s", "n_near", "n_far", "n_par", "st"]
+              + ["ld_c%d" % i for i in range(len(C_PARTS))]
+              + [x + p for x in ("q_", "s_") for p in SENT]
+              + [x + p for x in ("v_", "a_") for p in list(SENT) + list(MINE)]
+              + ["mm_" + p[0] for p in PRODUCTS] + ["cp_" + p for p in LAND]
+              + [x + "%d" % i for x in ("v_y", "a_y") for i in range(len(Y_STEPS))])
 
 
 def mask_of(engines):
     return sum(1 << e for e in engines)
+
+
+def u8(view):
+    return view.bitcast(dt.uint8)
 
 
 def plan(T, topo, r):
@@ -61,31 +79,33 @@ def plan(T, topo, r):
     near = r ^ 1
     far = [q for q in mates if q not in (par, near)][0]
     own = [c for c in topo.cores_of(me) if c != me]
-    hnear = [c for c in own if topo.may_write(c, T.cores[near]) and topo.die(c) == topo.die(me)][:2]
-    hfar = [c for c in own if topo.may_write(c, T.cores[far]) and topo.die(c) != topo.die(me)][:2]
+    hnear = [c for c in own if topo.may_write(c, T.cores[near]) and topo.die(c) == topo.die(me)][0]
+    hfar = [c for c in own if topo.may_write(c, T.cores[far]) and topo.die(c) != topo.die(me)][0]
     return {"near": near, "far": far, "par": par, "hnear": hnear, "hfar": hfar}
 
 
-def helper_program(g, core, T, topo, r, role, pl):
+def helper_program(g, core, T, topo, role, pl):
     S = T.sem
-    dst, par = T.cores[pl[role]], T.cores[pl["par"]]
-    rid, pid = topo.addr(dst, core)
-    m = mask_of(topo.engines(core, dst)[:8])
-    b = (r % PER) * BLK
-    slot = PEERS.index(role) * K
-    if core == pl["h" + role][0]:
-        g.wait_ge(S.h_n, 8)
-        g.remote_dma(T.nland[:, slot:slot + K], T.hn[:], S["n_" + role], S.sent, pid, rid, m)
-        g.wait_ge(S.h_d, 16)
-        g.remote_dma(T.landq[:, b:b + BLK].bitcast(dt.uint8), T.hq[:, 0:BLK].bitcast(dt.uint8), S["q_" + role], S.sent, pid, rid, m)
+    n = [0]
+
+    def hand_on(sem, count, dst_rank, out, in_, rsem):
+        dst = T.cores[dst_rank]
+        rid, pid = topo.addr(dst, core)
+        eng = topo.engines(core, dst)
+        g.wait_ge(sem, count)
+        g.remote_dma(out, in_, rsem, S.sent, pid, rid, mask_of(eng))
+        n[0] += len(eng)
+
+    p = LAND.index(role) * CR
+    hand_on(S.h_raw, 1, pl["par"], T.praw[0 if role == "near" else 1], T.hraw[:], S.raw_in)
+    hand_on(S.h_n, 4, pl[role], T["n" + role][:, 0:LN], T.hn[:], S["n_" + role])
+    if role == "far":
+        hand_on(S.h_o, 8, pl["far"], u8(T.wrq[:, 0:UN]), u8(T.hoq[:, 0:UN]), S.r_q)
     else:
-        prid, ppid = topo.addr(par, core)
-        e = 2 * K + (0 if role == "near" else LN)
-        g.wait_ge(S.h_n, 4)
-        g.remote_dma(T.nland[:, e:e + LN], T.hp[:], S.n_par, S.sent, ppid, prid, mask_of(topo.engines(core, par)[:8]))
-        g.wait_ge(S.h_d, 8)
-        g.remote_dma(T.lands[:, b:b + BLK], T.hs[:, 0:BLK], S["s_" + role], S.sent, pid, rid, m)
-    g.wait_ge(S.sent, 16)
+        hand_on(S.h_o, 8, pl["far"], T.wrs[:, 0:UN], T.hos[:, 0:UN], S.r_s)
+    hand_on(S.h_q, 16, pl[role], u8(T.landq[:, p:p + CR]), u8(T.hq[:, 0:CR]), S["q_" + role])
+    hand_on(S.h_s, 8, pl[role], T.lands[:, p:p + CR], T.hs[:, 0:CR], S["s_" + role])
+    g.wait_ge(S.sent, n[0])
 
 
 def rank_program(g, core, T, topo):
@@ -95,185 +115,195 @@ def rank_program(g, core, T, topo):
             if core in topo.cores_of(T.cores[q]):
                 pl = plan(T, topo, q)
                 for role in ("near", "far"):
-                    if core in pl["h" + role]:
-                        helper_program(g, core, T, topo, q, role, pl)
+                    if core == pl["h" + role]:
+                        helper_program(g, core, T, topo, role, pl)
         return
     S = T.sem
     v, a, te, sy = g.vector, g.scalar, g.tensor, g.sync
     COPY = ActivationFunctionType.Copy
     pl = plan(T, topo, r)
-    h, b = r // PER, r % PER
-    own0 = h * UN
-    xh = T.cores[(r + PER) % N]
+    h = r // PER
 
-    for i in range(8):
-        (sy if i % 2 == 0 else a).dma_start(T.needs[16 * i:16 * i + 16, :, :], T.need[:]).then_inc(S.ld_need, 16)
-    for i in range(2):
-        a.dma_start(T.ct[:, 2 * T_COLS * i:2 * T_COLS * (i + 1)], T.c[:, 2 * T_COLS * i:2 * T_COLS * (i + 1)]).then_inc(S["ld_c%d" % i], 16)
-    for i in range(8):
-        (sy if i % 2 == 0 else a).dma_start(T.unis[16 * i:16 * i + 16, :], T.uni[:]).then_inc(S.ld_uni, 16)
-    sy.wait_ge(S.ld_need, 128)
+    def across(q):
+        return (q + PER) % N
+
+    owner = {"near": across(pl["near"]), "far": across(pl["far"]), "paro": pl["par"], "parx": across(pl["par"]),
+             "relay": pl["near"], "meo": r, "mex": across(r), "mer": pl["far"]}
+
+    sy.dma_start(T.raw[:], T.need[:]).then_inc(S.ld_raw, 16)
+    for i, q_ in enumerate((a, sy)):
+        q_.dma_start(T.needs[16 * i:16 * i + 16, :, :], T.need[:]).then_inc(S.ld_need, 16)
+        q_.dma_start(T.unis[16 * i:16 * i + 16, :], T.uni[:]).then_inc(S.ld_uni, 16)
+    for i, (c0, c1) in enumerate(C_PARTS):
+        a.dma_start(T.ct[:, 4 * c0:4 * c1], T.c[:, 4 * c0:4 * c1]).then_inc(S["ld_c%d" % i], 16)
+    sy.wait_ge(S.l_sent, 8)
     sy.dma_start(T.wt[:], T.w[:]).then_inc(S.ld_w, 16)
     for i in range(8):
         sy.dma_start(T.poss[16 * i:16 * i + 16, :], T.pos[:]).then_inc(S.ld_pos, 16)
+    sy.wait_ge(S.raw_in, 16)
+    sy.dma_start(T.rels[0:32, :], T.praw[:, pl["far"]:128:N, :]).then_inc(S.ld_rel, 16)
 
-    def offs(who):
-        if who == "me":
-            return T.nown[:, 0:K]
-        e = PEERS.index(who) * K
-        return T.nland[:, e:e + K]
-
-    def place(who):
-        return (b if who == "me" else PEERS.index(who)) * BLK
+    def where(who):
+        if who in SENT:
+            return SENT[who], T["n" + who][:, 0:LN], T.vq, T.vs, list(SENT).index(who) * CR
+        return MINE[who], T.nl[:, owner[who], 0:LN], T.landq, T.lands, LAND.index(who) * CR
 
     def pick_codes(who):
-        p, out = place(who), T.landq if who == "me" else T.vq
-        v.tensor_copy(out[:, p:p + BLK].bitcast(dt.uint32), T.winq[:, 0:2 * UN].bitcast(dt.uint32).indirect(offs(who))).then_inc(S["v_" + who], 1)
+        w_, offs, out, _, p = where(who)
+        v.tensor_copy(out[:, p:p + CR].bitcast(dt.uint32), T["w%sq" % w_][:, 0:UN].bitcast(dt.uint32).indirect(offs)).then_inc(S["v_" + who], 1)
 
     def pick_scales(who):
-        p, out = place(who), T.lands if who == "me" else T.vs
-        a.activation(out[:, p:p + BLK], T.wins[:, 0:2 * UN].indirect(offs(who)), COPY).then_inc(S["a_" + who], 1)
+        w_, offs, _, out, p = where(who)
+        a.activation(out[:, p:p + CR], T["w%ss" % w_][:, 0:UN].indirect(offs), COPY).then_inc(S["a_" + who], 1)
 
-    v.wait_ge(S.ld_need, 128)
-    v.tensor_copy(T.nlist[:, :, 0:LN], T.needs[:, 0:PER, :]).then_inc(S.v_n0, 1)
-    v.tensor_scalar(T.nlist[:, :, LN:K], T.needs[:, PER:N, :], float(UN), None, AluOpType.add).then_inc(S.v_n1, 1)
-    hc = T_COLS // 2
-    v.wait_ge(S.ld_c0, 16)
-    v.quantize_mx(T.cq[:, 0:hc], T.cs[:, 0:hc], T.ct[:, 0:4 * hc]).then_inc(S.v_qc, 1)
-    v.wait_ge(S.ld_uni, 128)
-    v.tensor_copy(T.uoff[:], T.unis[:]).then_inc(S.v_u, 1)
-    v.wait_ge(S.ld_c1, 16)
-    v.quantize_mx(T.cq[:, hc:T_COLS], T.cs[:, hc:T_COLS], T.ct[:, 4 * hc:4 * T_COLS]).then_inc(S.v_qc, 1)
+    v.wait_ge(S.ld_need, 32)
+    for k in range(4):
+        v.tensor_copy(T.nl[32 * k:32 * k + 32, :, 0:LN], T.needs[0:32, :, :]).then_inc(S.v_n, 1)
+    v.wait_ge(S.ld_uni, 32)
+    for k in range(4):
+        v.tensor_copy(T.uoff[32 * k:32 * k + 32, :], T.unis[0:32, :]).then_inc(S.v_u, 1)
+    for i, (c0, c1) in enumerate(C_PARTS):
+        v.wait_ge(S["ld_c%d" % i], 16)
+        v.quantize_mx(T.cq[:, c0:c1], T.cs[:, c0:c1], T.ct[:, 4 * c0:4 * c1]).then_inc(S.v_qc, 1)
     uoth, uown = T.uoff[:, (1 - h) * LU:(2 - h) * LU], T.uoff[:, h * LU:(h + 1) * LU]
-    v.wait_ge(S.v_u, 1)
-    v.wait_ge(S.v_qc, 2)
+    v.wait_ge(S.v_u, 4)
+    v.wait_ge(S.v_qc, len(C_PARTS))
     v.tensor_copy(T.xq[:, 0:UN].bitcast(dt.uint32), T.cq[:, 0:T_COLS].bitcast(dt.uint32).indirect(uoth)).then_inc(S.v_xq, 1)
-    v.tensor_copy(T.winq[:, own0:own0 + UN].bitcast(dt.uint32), T.cq[:, 0:T_COLS].bitcast(dt.uint32).indirect(uown)).then_inc(S.v_wq, 1)
-    v.tensor_copy(T.nown[:, 0:LN], T.needs[:, b, :]).then_inc(S.v_o0, 1)
-    v.tensor_scalar(T.nown[:, LN:K], T.needs[:, PER + b, :], float(UN), None, AluOpType.add).then_inc(S.v_o1, 1)
-    v.wait_ge(S.v_wq, 1)
+    v.tensor_copy(T.woq[:, 0:UN].bitcast(dt.uint32), T.cq[:, 0:T_COLS].bitcast(dt.uint32).indirect(uown)).then_inc(S.v_oq, 1)
+    v.wait_ge(S.v_oq, 1)
+    v.wait_ge(S.v_n, 4)
+    v.wait_ge(S.n_par, 8)
+    pick_codes("paro")
+    pick_codes("meo")
     v.wait_ge(S.x_q, 8)
     v.wait_ge(S.n_near, 8)
     pick_codes("near")
     v.wait_ge(S.n_far, 8)
     pick_codes("far")
-    v.wait_ge(S.n_par, 16)
-    pick_codes("par")
-    v.wait_ge(S.v_o0, 1)
-    v.wait_ge(S.v_o1, 1)
-    pick_codes("me")
+    pick_codes("parx")
+    pick_codes("mex")
     v.wait_ge(S.ld_w, 16)
     v.quantize_mx(T.wq[:, 0:128], T.ws[:, 0:128], T.wt[:, 0:512]).then_inc(S.v_qw, 1)
-    GE, MUL, ADD = AluOpType.is_ge, AluOpType.mult, AluOpType.add
     v.wait_ge(S.ld_pos, 128)
-    v.tensor_scalar(T.pa[:], T.poss[:], float(PER * CR), float(PER * CR), GE, MUL).then_inc(S.v_p0, 1)
-    v.tensor_scalar(T.b4[:], T.poss[:], float(PER * CR), float(CR), GE, MUL).then_inc(S.v_p1, 1)
-    v.wait_ge(S.v_p0, 1)
-    v.tensor_tensor(T.pb[:], T.poss[:], T.pa[:], AluOpType.subtract).then_inc(S.v_p2, 1)
-    v.wait_ge(S.v_p2, 1)
-    v.tensor_scalar(T.b1[:], T.pb[:], float(CR), float(CR), GE, MUL).then_inc(S.v_p3, 1)
-    v.tensor_scalar(T.b2[:], T.pb[:], float(2 * CR), float(CR), GE, MUL).then_inc(S.v_p4, 1)
-    v.tensor_scalar(T.b3[:], T.pb[:], float(3 * CR), float(CR), GE, MUL).then_inc(S.v_p5, 1)
-    v.wait_ge(S.v_p3, 1)
-    v.wait_ge(S.v_p4, 1)
-    v.tensor_tensor(T.s1[:], T.b1[:], T.b2[:], ADD).then_inc(S.v_p6, 1)
-    v.wait_ge(S.v_p1, 1)
-    v.wait_ge(S.v_p5, 1)
-    v.tensor_tensor(T.s2[:], T.b3[:], T.b4[:], ADD).then_inc(S.v_p7, 1)
-    v.wait_ge(S.v_p6, 1)
-    v.wait_ge(S.v_p7, 1)
-    v.tensor_tensor(T.s3[:], T.s1[:], T.s2[:], ADD).then_inc(S.v_p8, 1)
-    v.wait_ge(S.v_p8, 1)
-    v.tensor_tensor(T.pa[:], T.s3[:], T.pb[:], ADD).then_inc(S.v_p9, 1)
-    v.wait_ge(S.v_p9, 1)
-    v.tensor_copy(T.poff[:], T.pa[:]).then_inc(S.v_po, 1)
+    v.tensor_copy(T.poff[:], T.poss[:]).then_inc(S.v_po, 1)
+    v.wait_ge(S.ld_rel, 16)
+    for k in range(4):
+        v.tensor_copy(T.nrelay[32 * k:32 * k + 32, 0:LN], T.rels[0:32, :]).then_inc(S.v_rel, 1)
+    v.wait_ge(S.v_rel, 4)
+    v.wait_ge(S.r_q, 8)
+    pick_codes("relay")
+    pick_codes("mer")
 
-    a.wait_ge(S.v_u, 1)
-    a.wait_ge(S.v_qc, 2)
+    a.wait_ge(S.v_u, 4)
+    a.wait_ge(S.v_qc, len(C_PARTS))
     a.activation(T.xs[:, 0:UN], T.cs[:, 0:T_COLS].indirect(uoth), COPY).then_inc(S.a_xs, 1)
-    a.activation(T.wins[:, own0:own0 + UN], T.cs[:, 0:T_COLS].indirect(uown), COPY).then_inc(S.a_ws, 1)
-    a.wait_ge(S.a_ws, 1)
+    a.activation(T.wos[:, 0:UN], T.cs[:, 0:T_COLS].indirect(uown), COPY).then_inc(S.a_os, 1)
+    a.wait_ge(S.a_os, 1)
+    a.wait_ge(S.v_n, 4)
+    a.wait_ge(S.n_par, 8)
+    pick_scales("paro")
+    pick_scales("meo")
     a.wait_ge(S.x_s, 8)
     a.wait_ge(S.n_near, 8)
     pick_scales("near")
     a.wait_ge(S.n_far, 8)
     pick_scales("far")
-    a.wait_ge(S.n_par, 16)
-    pick_scales("par")
-    a.wait_ge(S.v_o0, 1)
-    a.wait_ge(S.v_o1, 1)
-    pick_scales("me")
+    pick_scales("parx")
+    pick_scales("mex")
+    a.wait_ge(S.v_rel, 4)
+    a.wait_ge(S.r_s, 8)
+    pick_scales("relay")
+    pick_scales("mer")
 
-    def did(dst):
+    n = [0]
+
+    def send(dst, eng, out, in_, rsem):
         rid, pid = topo.addr(dst, core)
-        return [DstId(rid=rid, pnc=pid)]
+        g.remote_dma(out, in_, rsem, S.sent, pid, rid, mask_of(eng))
+        n[0] += len(eng)
 
-    hn, hf, sp = pl["hnear"], pl["hfar"], T.cores[pl["par"]]
-    en, ef = topo.engines(core, hn[0]), topo.engines(core, hf[0])
-    mp, mx = mask_of(topo.engines(core, sp)[:8]), mask_of(topo.engines(core, xh)[:8])
-    half = len(en) // 2
-    nd, fd, pd = pl["near"] % PER, pl["far"] % PER, pl["par"] % PER
-    g.wait_ge(S.v_n0, 1)
-    g.wait_ge(S.v_n1, 1)
-    for d, hc_ in ((nd, hn[0]), (fd, hf[0])):
-        hrid, hpid = topo.addr(hc_, core)
-        g.remote_dma(T.hn[:], T.nlist[:, d, :], S.h_n, S.sent, hpid, hrid, mask_of(topo.engines(core, hc_)[half:]))
-    g.remote_dma_fused([
-        RemoteDMATransfer(dst_ids=did(hn[1]), dma_engine_mask=mask_of(en[0:4]), remote_sem=S.h_n, src=T.nlist[:, pd, 0:LN], dst=T.hp[:]),
-        RemoteDMATransfer(dst_ids=did(hf[1]), dma_engine_mask=mask_of(ef[4:8]), remote_sem=S.h_n, src=T.nlist[:, pd, LN:K], dst=T.hp[:]),
-    ], local_sem=S.sent)
-    xrid, xpid = topo.addr(xh, core)
+    def fused(items, lsem=None):
+        ts = []
+        for dst, eng, out, in_, rsem in items:
+            rid, pid = topo.addr(dst, core)
+            ts.append(RemoteDMATransfer(dst_ids=[DstId(rid=rid, pnc=pid)], dma_engine_mask=mask_of(eng), remote_sem=rsem, src=in_, dst=out))
+            if lsem is None:
+                n[0] += len(eng)
+        g.remote_dma_fused(ts, local_sem=S.sent if lsem is None else lsem)
+
+    hn, hf, sp, xh = pl["hnear"], pl["hfar"], T.cores[pl["par"]], T.cores[across(r)]
+    off = topo.engines(core, sp)
+    on = topo.engines(core, hn)
+    rest = [e for e in on if e not in off]
+    lo, hi = rest[:len(rest) // 2], rest[len(rest) // 2:]
+    g.wait_ge(S.ld_raw, 16)
+    fused([(hn, lo[:1], T.hraw[:], T.raw[:], S.h_raw), (hf, hi[:1], T.hraw[:], T.raw[:], S.h_raw)])
+    g.wait_ge(S.v_n, 4)
+    fused([(hn, lo, T.hn[:], T.nl[:, owner["near"], 0:LN], S.h_n), (hf, hi, T.hn[:], T.nl[:, owner["far"], 0:LN], S.h_n)], S.l_sent)
+    fused([(sp, off[:4], T.nparo[:, 0:LN], T.nl[:, owner["paro"], 0:LN], S.n_par),
+           (sp, off[4:], T.nparx[:, 0:LN], T.nl[:, owner["parx"], 0:LN], S.n_par)])
     g.wait_ge(S.v_xq, 1)
-    g.remote_dma(T.winq[:, own0:own0 + UN].bitcast(dt.uint8), T.xq[:, 0:UN].bitcast(dt.uint8), S.x_q, S.sent, xpid, xrid, mx)
+    send(xh, off, u8(T.wxq[:, 0:UN]), u8(T.xq[:, 0:UN]), S.x_q)
     g.wait_ge(S.a_xs, 1)
-    g.remote_dma(T.wins[:, own0:own0 + UN], T.xs[:, 0:UN], S.x_s, S.sent, xpid, xrid, mx)
-    to = {"far": (hf, ef[half:]), "near": (hn, en[:half])}
-    for who in ("near", "far"):
-        p, hc_ = place(who), to[who][0][0]
-        hrid, hpid = topo.addr(hc_, core)
+    send(xh, off, T.wxs[:, 0:UN], T.xs[:, 0:UN], S.x_s)
+    g.wait_ge(S.v_oq, 1)
+    send(hf, rest, u8(T.hoq[:, 0:UN]), u8(T.woq[:, 0:UN]), S.h_o)
+    g.wait_ge(S.a_os, 1)
+    send(hn, rest, T.hos[:, 0:UN], T.wos[:, 0:UN], S.h_o)
+
+    def to_par(who):
+        p, l = list(SENT).index(who) * CR, LAND.index(who) * CR
         g.wait_ge(S["v_" + who], 1)
-        g.remote_dma(T.hq[:, 0:BLK].bitcast(dt.uint8), T.vq[:, p:p + BLK].bitcast(dt.uint8), S.h_d, S.sent, hpid, hrid, mask_of(topo.engines(core, hc_)))
-    for who in ("near", "far"):
-        p, hs_ = place(who), to[who][0][1]
-        hrid, hpid = topo.addr(hs_, core)
+        send(sp, off, u8(T.landq[:, l:l + CR]), u8(T.vq[:, p:p + CR]), S["q_" + who])
         g.wait_ge(S["a_" + who], 1)
-        g.remote_dma(T.hs[:, 0:BLK], T.vs[:, p:p + BLK], S.h_d, S.sent, hpid, hrid, mask_of(to[who][1]))
-    rid, pid = topo.addr(sp, core)
-    g.wait_ge(S.v_par, 1)
-    g.remote_dma(T.landq[:, b * BLK:(b + 1) * BLK].bitcast(dt.uint8), T.vq[:, 2 * BLK:3 * BLK].bitcast(dt.uint8), S.q_par, S.sent, pid, rid, mp)
-    g.wait_ge(S.a_par, 1)
-    g.remote_dma(T.lands[:, b * BLK:(b + 1) * BLK], T.vs[:, 2 * BLK:3 * BLK], S.s_par, S.sent, pid, rid, mp)
-    g.wait_ge(S.sent, 104)
+        send(sp, off, T.lands[:, l:l + CR], T.vs[:, p:p + CR], S["s_" + who])
+
+    to_par("paro")
+    for who, hc in (("near", hn), ("far", hf)):
+        p = list(SENT).index(who) * CR
+        g.wait_ge(S["v_" + who], 1)
+        send(hc, on, u8(T.hq[:, 0:CR]), u8(T.vq[:, p:p + CR]), S.h_q)
+    g.wait_ge(S.a_near, 1)
+    g.wait_ge(S.a_far, 1)
+    fused([(hn, off, T.hs[:, 0:CR], T.vs[:, 0:CR], S.h_s), (hf, rest, T.hs[:, 0:CR], T.vs[:, CR:2 * CR], S.h_s)])
+    to_par("parx")
+    to_par("relay")
+    g.wait_ge(S.sent, n[0])
 
     te.wait_ge(S.v_qw, 1)
-    order = [(b, None), (pd, "par"), (nd, "near"), (fd, "far")]
-    for j, role in order:
-        if role is None:
-            te.wait_ge(S.v_me, 1)
-            te.wait_ge(S.a_me, 1)
-        else:
-            te.wait_ge(S["q_" + role], 8)
-            te.wait_ge(S["s_" + role], 8)
-        te.matmul_mx(T.ps[:, 512 * j:512 * j + BLK], T.wq[:, 0:128], T.ws[:, 0:128],
-                     T.landq[:, j * BLK:(j + 1) * BLK], T.lands[:, j * BLK:(j + 1) * BLK], True, True).then_inc(S["mm%d" % j], 1)
-    for j in (b, fd):
-        v.wait_ge(S["mm%d" % j], 1)
-        v.tensor_copy(T.res[:, j * BLK:(j + 1) * BLK], T.ps[:, 512 * j:512 * j + BLK]).then_inc(S["cp%d" % j], 1)
-    for j in (pd, nd):
-        a.wait_ge(S["mm%d" % j], 1)
-        a.activation(T.res[:, j * BLK:(j + 1) * BLK], T.ps[:, 512 * j:512 * j + BLK], COPY).then_inc(S["cp%d" % j], 1)
+    bank = {}
+    for j, (name, blocks, c0, cols) in enumerate(PRODUCTS):
+        for who in blocks:
+            if who in MINE:
+                te.wait_ge(S["v_" + who], 1)
+                te.wait_ge(S["a_" + who], 1)
+            else:
+                te.wait_ge(S["q_" + who], 8)
+                te.wait_ge(S["s_" + who], 8)
+            bank[who] = (name, 512 * j + LAND.index(who) * CR - c0)
+        te.matmul_mx(T.ps[:, 512 * j:512 * j + cols], T.wq[:, 0:128], T.ws[:, 0:128],
+                     T.landq[:, c0:c0 + cols], T.lands[:, c0:c0 + cols], True, True).then_inc(S["mm_" + name], 1)
+    for e, blocks in ((v, ["mer", "mex", "near", "relay"]), (a, ["meo", "paro", "parx", "far"])):
+        for who in blocks:
+            name, p = bank[who]
+            o = owner[who] * CR
+            e.wait_ge(S["mm_" + name], 1)
+            if e is v:
+                v.tensor_copy(T.res[:, o:o + CR], T.ps[:, p:p + CR]).then_inc(S["cp_" + who], 1)
+            else:
+                a.activation(T.res[:, o:o + CR], T.ps[:, p:p + CR], COPY).then_inc(S["cp_" + who], 1)
     for e in (v, a):
         e.wait_ge(S.v_po, 1)
-        for j in range(PER):
-            e.wait_ge(S["cp%d" % j], 1)
-    win = T.res[:, 0:PER * BLK]
-    qw, qk = W // 4, W // 64
-    for i in range(2):
-        c0, k0 = 2 * i * qw, 2 * i * qk
-        v.tensor_copy(T.yt[:, c0:c0 + qw], win.indirect(T.poff[:, k0:k0 + qk])).then_inc(S["v_y%d" % i], 1)
-        a.activation(T.yt[:, c0 + qw:c0 + 2 * qw], win.indirect(T.poff[:, k0 + qk:k0 + 2 * qk]), COPY).then_inc(S["a_y%d" % i], 1)
+        for who in LAND:
+            e.wait_ge(S["cp_" + who], 1)
+    win = T.res[:, 0:N * CR]
+    c0 = 0
+    for i, cols in enumerate(Y_STEPS):
+        c1, c2 = c0 + cols, c0 + 2 * cols
+        v.tensor_copy(T.yt[:, c0:c1], win.indirect(T.poff[:, c0 // 16:c1 // 16])).then_inc(S["v_y%d" % i], 1)
+        a.activation(T.yt[:, c1:c2], win.indirect(T.poff[:, c1 // 16:c2 // 16]), COPY).then_inc(S["a_y%d" % i], 1)
         sy.wait_ge(S["v_y%d" % i], 1)
         sy.wait_ge(S["a_y%d" % i], 1)
-        sy.dma_start(T.y[:, c0:c0 + 2 * qw], T.yt[:, c0:c0 + 2 * qw]).then_inc(S["st%d" % i], 16)
-    for i in range(2):
-        sy.wait_ge(S["st%d" % i], 16)
+        sy.dma_start(T.y[:, c0:c2], T.yt[:, c0:c2]).then_inc(S.st, 16)
+        c0 = c2
+    sy.wait_ge(S.st, 16 * len(Y_STEPS))

from concourse.bass import DstId, RemoteDMATransfer
from concourse.mybir import dt, AluOpType, ActivationFunctionType

N, UN, CR, T_COLS, W = 8, 160, 80, 512, 512
PER = 4
LU, LN = UN // 16, CR // 16
LP = LN + 1
CODES, I32, U16, F32 = "float8_e4m3fn_x4", "int32", "uint16", "float32"
C_PARTS = [(0, 256), (256, 384), (384, 512)]
Y_STEPS = [64, 64, 128]
MM_MIN = 128

SENT = {"near": "x", "far": "x", "paro": "o", "parx": "x", "relay": "r"}
MINE = {"meo": "o", "mex": "x", "mer": "r"}
LAND = ["near", "meo", "paro", "far", "mer", "mex", "parx", "relay"]
PRODUCTS = [("e", ["meo", "paro"], CR, 2 * CR), ("m", ["mer", "mex"], 4 * CR, 2 * CR),
            ("parx", ["parx"], 7 * CR - MM_MIN, MM_MIN), ("near", ["near"], 0, MM_MIN),
            ("far", ["far"], 4 * CR - MM_MIN, MM_MIN), ("relay", ["relay"], 8 * CR - MM_MIN, MM_MIN)]

SCRATCH = {
    "raw": ("dram", [128, LN], I32),
    "hraw": ("dram", [128, LN], I32),
    "praw": ("dram", [2, 128, LN], I32),
    "needs": ("sbuf", [128, N, LN], I32),
    "nl": ("sbuf", [128, N, LP], U16),
    "rels": ("sbuf", [128, LN], I32),
    "unis": ("sbuf", [128, 2 * LU], I32),
    "uoff": ("sbuf", [128, 2 * LU], U16),
    "poss": ("sbuf", [128, W // 16], I32),
    "poff": ("sbuf", [128, W // 16], U16),
    "ct": ("sbuf", [128, 4 * T_COLS], "bfloat16"),
    "wt": ("sbuf", [128, 512], "bfloat16"),
    "cq": ("sbuf", [128, T_COLS], CODES),
    "cs": ("sbuf", [128, T_COLS], "uint8"),
    "wq": ("sbuf", [128, 128], CODES),
    "ws": ("sbuf", [128, 128], "uint8"),
    "xq": ("sbuf", [128, UN], CODES),
    "xs": ("sbuf", [128, UN], "uint8"),
    "vq": ("sbuf", [128, len(SENT) * CR], CODES),
    "vs": ("sbuf", [128, len(SENT) * CR], "uint8"),
    "landq": ("sbuf", [128, N * CR], CODES),
    "lands": ("sbuf", [128, N * CR], "uint8"),
    "hn": ("sbuf", [128, LN], U16),
    "hoq": ("sbuf", [128, UN], CODES),
    "hos": ("sbuf", [128, UN], "uint8"),
    "hq": ("sbuf", [128, CR], CODES),
    "hs": ("sbuf", [128, CR], "uint8"),
    "ps": ("psum", [128, 512 * len(PRODUCTS)], F32),
    "res": ("sbuf", [128, N * CR], F32),
    "yt": ("sbuf", [128, W], F32),
}
for n_ in "oxr":
    SCRATCH["w%sq" % n_] = ("sbuf", [128, UN], CODES)
    SCRATCH["w%ss" % n_] = ("sbuf", [128, UN], "uint8")
for n_ in SENT:
    SCRATCH["n" + n_] = ("sbuf", [128, LP], U16)
SEMAPHORES = (["ld_raw", "ld_need", "ld_uni", "ld_w", "ld_pos", "ld_rel", "sent", "l_sent", "raw_in",
               "v_n", "v_u", "v_rel", "v_qc", "v_qw", "v_po", "v_xq", "a_xs", "v_oq", "a_os",
               "x_q", "x_s", "r_q", "r_s", "h_raw", "h_n", "h_o", "h_q", "h_s", "n_near", "n_far", "n_par", "st"]
              + ["ld_c%d" % i for i in range(len(C_PARTS))]
              + [x + p for x in ("q_", "s_") for p in SENT]
              + [x + p for x in ("v_", "a_") for p in list(SENT) + list(MINE)]
              + ["mm_" + p[0] for p in PRODUCTS] + ["cp_" + p for p in LAND]
              + [x + "%d" % i for x in ("v_y", "a_y") for i in range(len(Y_STEPS))])


def mask_of(engines):
    return sum(1 << e for e in engines)


def u8(view):
    return view.bitcast(dt.uint8)


def plan(T, topo, r):
    me = T.cores[r]
    mates = [q for q in range(N) if topo.host(T.cores[q]) == topo.host(me) and q != r]
    par = [q for q in mates if topo.may_write(me, T.cores[q])][0]
    near = r ^ 1
    far = [q for q in mates if q not in (par, near)][0]
    own = [c for c in topo.cores_of(me) if c != me]
    hnear = [c for c in own if topo.may_write(c, T.cores[near]) and topo.die(c) == topo.die(me)][0]
    hfar = [c for c in own if topo.may_write(c, T.cores[far]) and topo.die(c) != topo.die(me)][0]
    return {"near": near, "far": far, "par": par, "hnear": hnear, "hfar": hfar}


def helper_program(g, core, T, topo, role, pl):
    S = T.sem
    n = [0]

    def hand_on(sem, count, dst_rank, out, in_, rsem):
        dst = T.cores[dst_rank]
        rid, pid = topo.addr(dst, core)
        eng = topo.engines(core, dst)
        g.wait_ge(sem, count)
        g.remote_dma(out, in_, rsem, S.sent, pid, rid, mask_of(eng))
        n[0] += len(eng)

    p = LAND.index(role) * CR
    hand_on(S.h_raw, 1, pl["par"], T.praw[0 if role == "near" else 1], T.hraw[:], S.raw_in)
    hand_on(S.h_n, 4, pl[role], T["n" + role][:, 0:LN], T.hn[:], S["n_" + role])
    if role == "far":
        hand_on(S.h_o, 8, pl["far"], u8(T.wrq[:, 0:UN]), u8(T.hoq[:, 0:UN]), S.r_q)
    else:
        hand_on(S.h_o, 8, pl["far"], T.wrs[:, 0:UN], T.hos[:, 0:UN], S.r_s)
    hand_on(S.h_q, 16, pl[role], u8(T.landq[:, p:p + CR]), u8(T.hq[:, 0:CR]), S["q_" + role])
    hand_on(S.h_s, 8, pl[role], T.lands[:, p:p + CR], T.hs[:, 0:CR], S["s_" + role])
    g.wait_ge(S.sent, n[0])


def rank_program(g, core, T, topo):
    r = T.rank_of(core)
    if r is None:
        for q in range(N):
            if core in topo.cores_of(T.cores[q]):
                pl = plan(T, topo, q)
                for role in ("near", "far"):
                    if core == pl["h" + role]:
                        helper_program(g, core, T, topo, role, pl)
        return
    S = T.sem
    v, a, te, sy = g.vector, g.scalar, g.tensor, g.sync
    COPY = ActivationFunctionType.Copy
    pl = plan(T, topo, r)
    h = r // PER

    def across(q):
        return (q + PER) % N

    owner = {"near": across(pl["near"]), "far": across(pl["far"]), "paro": pl["par"], "parx": across(pl["par"]),
             "relay": pl["near"], "meo": r, "mex": across(r), "mer": pl["far"]}

    sy.dma_start(T.raw[:], T.need[:]).then_inc(S.ld_raw, 16)
    for i, q_ in enumerate((a, sy)):
        q_.dma_start(T.needs[16 * i:16 * i + 16, :, :], T.need[:]).then_inc(S.ld_need, 16)
        q_.dma_start(T.unis[16 * i:16 * i + 16, :], T.uni[:]).then_inc(S.ld_uni, 16)
    for i, (c0, c1) in enumerate(C_PARTS):
        a.dma_start(T.ct[:, 4 * c0:4 * c1], T.c[:, 4 * c0:4 * c1]).then_inc(S["ld_c%d" % i], 16)
    sy.wait_ge(S.l_sent, 8)
    sy.dma_start(T.wt[:], T.w[:]).then_inc(S.ld_w, 16)
    for i in range(8):
        sy.dma_start(T.poss[16 * i:16 * i + 16, :], T.pos[:]).then_inc(S.ld_pos, 16)
    sy.wait_ge(S.raw_in, 16)
    sy.dma_start(T.rels[0:32, :], T.praw[:, pl["far"]:128:N, :]).then_inc(S.ld_rel, 16)

    def where(who):
        if who in SENT:
            return SENT[who], T["n" + who][:, 0:LN], T.vq, T.vs, list(SENT).index(who) * CR
        return MINE[who], T.nl[:, owner[who], 0:LN], T.landq, T.lands, LAND.index(who) * CR

    def pick_codes(who):
        w_, offs, out, _, p = where(who)
        v.tensor_copy(out[:, p:p + CR].bitcast(dt.uint32), T["w%sq" % w_][:, 0:UN].bitcast(dt.uint32).indirect(offs)).then_inc(S["v_" + who], 1)

    def pick_scales(who):
        w_, offs, _, out, p = where(who)
        a.activation(out[:, p:p + CR], T["w%ss" % w_][:, 0:UN].indirect(offs), COPY).then_inc(S["a_" + who], 1)

    v.wait_ge(S.ld_need, 32)
    for k in range(4):
        v.tensor_copy(T.nl[32 * k:32 * k + 32, :, 0:LN], T.needs[0:32, :, :]).then_inc(S.v_n, 1)
    v.wait_ge(S.ld_uni, 32)
    for k in range(4):
        v.tensor_copy(T.uoff[32 * k:32 * k + 32, :], T.unis[0:32, :]).then_inc(S.v_u, 1)
    for i, (c0, c1) in enumerate(C_PARTS):
        v.wait_ge(S["ld_c%d" % i], 16)
        v.quantize_mx(T.cq[:, c0:c1], T.cs[:, c0:c1], T.ct[:, 4 * c0:4 * c1]).then_inc(S.v_qc, 1)
    uoth, uown = T.uoff[:, (1 - h) * LU:(2 - h) * LU], T.uoff[:, h * LU:(h + 1) * LU]
    v.wait_ge(S.v_u, 4)
    v.wait_ge(S.v_qc, len(C_PARTS))
    v.tensor_copy(T.xq[:, 0:UN].bitcast(dt.uint32), T.cq[:, 0:T_COLS].bitcast(dt.uint32).indirect(uoth)).then_inc(S.v_xq, 1)
    v.tensor_copy(T.woq[:, 0:UN].bitcast(dt.uint32), T.cq[:, 0:T_COLS].bitcast(dt.uint32).indirect(uown)).then_inc(S.v_oq, 1)
    v.wait_ge(S.v_oq, 1)
    v.wait_ge(S.v_n, 4)
    v.wait_ge(S.n_par, 8)
    pick_codes("paro")
    pick_codes("meo")
    v.wait_ge(S.x_q, 8)
    v.wait_ge(S.n_near, 8)
    pick_codes("near")
    v.wait_ge(S.n_far, 8)
    pick_codes("far")
    pick_codes("parx")
    pick_codes("mex")
    v.wait_ge(S.ld_w, 16)
    v.quantize_mx(T.wq[:, 0:128], T.ws[:, 0:128], T.wt[:, 0:512]).then_inc(S.v_qw, 1)
    v.wait_ge(S.ld_pos, 128)
    v.tensor_copy(T.poff[:], T.poss[:]).then_inc(S.v_po, 1)
    v.wait_ge(S.ld_rel, 16)
    for k in range(4):
        v.tensor_copy(T.nrelay[32 * k:32 * k + 32, 0:LN], T.rels[0:32, :]).then_inc(S.v_rel, 1)
    v.wait_ge(S.v_rel, 4)
    v.wait_ge(S.r_q, 8)
    pick_codes("relay")
    pick_codes("mer")

    a.wait_ge(S.v_u, 4)
    a.wait_ge(S.v_qc, len(C_PARTS))
    a.activation(T.xs[:, 0:UN], T.cs[:, 0:T_COLS].indirect(uoth), COPY).then_inc(S.a_xs, 1)
    a.activation(T.wos[:, 0:UN], T.cs[:, 0:T_COLS].indirect(uown), COPY).then_inc(S.a_os, 1)
    a.wait_ge(S.a_os, 1)
    a.wait_ge(S.v_n, 4)
    a.wait_ge(S.n_par, 8)
    pick_scales("paro")
    pick_scales("meo")
    a.wait_ge(S.x_s, 8)
    a.wait_ge(S.n_near, 8)
    pick_scales("near")
    a.wait_ge(S.n_far, 8)
    pick_scales("far")
    pick_scales("parx")
    pick_scales("mex")
    a.wait_ge(S.v_rel, 4)
    a.wait_ge(S.r_s, 8)
    pick_scales("relay")
    pick_scales("mer")

    n = [0]

    def send(dst, eng, out, in_, rsem):
        rid, pid = topo.addr(dst, core)
        g.remote_dma(out, in_, rsem, S.sent, pid, rid, mask_of(eng))
        n[0] += len(eng)

    def fused(items, lsem=None):
        ts = []
        for dst, eng, out, in_, rsem in items:
            rid, pid = topo.addr(dst, core)
            ts.append(RemoteDMATransfer(dst_ids=[DstId(rid=rid, pnc=pid)], dma_engine_mask=mask_of(eng), remote_sem=rsem, src=in_, dst=out))
            if lsem is None:
                n[0] += len(eng)
        g.remote_dma_fused(ts, local_sem=S.sent if lsem is None else lsem)

    hn, hf, sp, xh = pl["hnear"], pl["hfar"], T.cores[pl["par"]], T.cores[across(r)]
    off = topo.engines(core, sp)
    on = topo.engines(core, hn)
    rest = [e for e in on if e not in off]
    lo, hi = rest[:len(rest) // 2], rest[len(rest) // 2:]
    g.wait_ge(S.ld_raw, 16)
    fused([(hn, lo[:1], T.hraw[:], T.raw[:], S.h_raw), (hf, hi[:1], T.hraw[:], T.raw[:], S.h_raw)])
    g.wait_ge(S.v_n, 4)
    fused([(hn, lo, T.hn[:], T.nl[:, owner["near"], 0:LN], S.h_n), (hf, hi, T.hn[:], T.nl[:, owner["far"], 0:LN], S.h_n)], S.l_sent)
    fused([(sp, off[:4], T.nparo[:, 0:LN], T.nl[:, owner["paro"], 0:LN], S.n_par),
           (sp, off[4:], T.nparx[:, 0:LN], T.nl[:, owner["parx"], 0:LN], S.n_par)])
    g.wait_ge(S.v_xq, 1)
    send(xh, off, u8(T.wxq[:, 0:UN]), u8(T.xq[:, 0:UN]), S.x_q)
    g.wait_ge(S.a_xs, 1)
    send(xh, off, T.wxs[:, 0:UN], T.xs[:, 0:UN], S.x_s)
    g.wait_ge(S.v_oq, 1)
    send(hf, rest, u8(T.hoq[:, 0:UN]), u8(T.woq[:, 0:UN]), S.h_o)
    g.wait_ge(S.a_os, 1)
    send(hn, rest, T.hos[:, 0:UN], T.wos[:, 0:UN], S.h_o)

    def to_par(who):
        p, l = list(SENT).index(who) * CR, LAND.index(who) * CR
        g.wait_ge(S["v_" + who], 1)
        send(sp, off, u8(T.landq[:, l:l + CR]), u8(T.vq[:, p:p + CR]), S["q_" + who])
        g.wait_ge(S["a_" + who], 1)
        send(sp, off, T.lands[:, l:l + CR], T.vs[:, p:p + CR], S["s_" + who])

    to_par("paro")
    for who, hc in (("near", hn), ("far", hf)):
        p = list(SENT).index(who) * CR
        g.wait_ge(S["v_" + who], 1)
        send(hc, on, u8(T.hq[:, 0:CR]), u8(T.vq[:, p:p + CR]), S.h_q)
    g.wait_ge(S.a_near, 1)
    g.wait_ge(S.a_far, 1)
    fused([(hn, off, T.hs[:, 0:CR], T.vs[:, 0:CR], S.h_s), (hf, rest, T.hs[:, 0:CR], T.vs[:, CR:2 * CR], S.h_s)])
    to_par("parx")
    to_par("relay")
    g.wait_ge(S.sent, n[0])

    te.wait_ge(S.v_qw, 1)
    bank = {}
    for j, (name, blocks, c0, cols) in enumerate(PRODUCTS):
        for who in blocks:
            if who in MINE:
                te.wait_ge(S["v_" + who], 1)
                te.wait_ge(S["a_" + who], 1)
            else:
                te.wait_ge(S["q_" + who], 8)
                te.wait_ge(S["s_" + who], 8)
            bank[who] = (name, 512 * j + LAND.index(who) * CR - c0)
        te.matmul_mx(T.ps[:, 512 * j:512 * j + cols], T.wq[:, 0:128], T.ws[:, 0:128],
                     T.landq[:, c0:c0 + cols], T.lands[:, c0:c0 + cols], True, True).then_inc(S["mm_" + name], 1)
    for e, blocks in ((v, ["mer", "mex", "near", "relay"]), (a, ["meo", "paro", "parx", "far"])):
        for who in blocks:
            name, p = bank[who]
            o = owner[who] * CR
            e.wait_ge(S["mm_" + name], 1)
            if e is v:
                v.tensor_copy(T.res[:, o:o + CR], T.ps[:, p:p + CR]).then_inc(S["cp_" + who], 1)
            else:
                a.activation(T.res[:, o:o + CR], T.ps[:, p:p + CR], COPY).then_inc(S["cp_" + who], 1)
    for e in (v, a):
        e.wait_ge(S.v_po, 1)
        for who in LAND:
            e.wait_ge(S["cp_" + who], 1)
    win = T.res[:, 0:N * CR]
    c0 = 0
    for i, cols in enumerate(Y_STEPS):
        c1, c2 = c0 + cols, c0 + 2 * cols
        v.tensor_copy(T.yt[:, c0:c1], win.indirect(T.poff[:, c0 // 16:c1 // 16])).then_inc(S["v_y%d" % i], 1)
        a.activation(T.yt[:, c1:c2], win.indirect(T.poff[:, c1 // 16:c2 // 16]), COPY).then_inc(S["a_y%d" % i], 1)
        sy.wait_ge(S["v_y%d" % i], 1)
        sy.wait_ge(S["a_y%d" % i], 1)
        sy.dma_start(T.y[:, c0:c2], T.yt[:, c0:c2]).then_inc(S.st, 16)
        c0 = c2
    sy.wait_ge(S.st, 16 * len(Y_STEPS))
